import numpy as np
import ml_dtypes


def mxq(x, axis, fmt="e4m3"):
    dtype, down = {"e4m3": (ml_dtypes.float8_e4m3fn, 7), "e5m2": (ml_dtypes.float8_e5m2, 14)}[fmt]
    v = np.moveaxis(np.asarray(x, np.float32).astype(ml_dtypes.bfloat16).astype(np.float64), axis, -1)
    blocks = v.reshape(v.shape[:-1] + (-1, 32))
    amax = np.abs(blocks).max(-1, keepdims=True)
    byte = np.maximum(np.where(amax > 0, np.frexp(amax)[1] - 1 + 127, 0) - down, 1)
    scale = np.exp2(byte - 127.0)
    codes = (blocks / scale).astype(np.float32).astype(dtype).astype(np.float64)
    return np.moveaxis((codes * scale).reshape(v.shape), -1, axis)


WIDE = False


def mx_kscale(k):
    if not WIDE:
        return np.ones(k)
    levels = np.array([10, -10, 5, -5, 0])
    if k % 512:
        return np.exp2(np.random.permutation(np.resize(levels, k // 32))).repeat(32)
    a = np.empty((k // 512, 16))
    for p in range(k // 512):
        a[p, :8] = np.random.permutation(np.resize(levels, 8))
        for g in range(8):
            far = levels[np.abs(levels - a[p, g]) >= 10]
            a[p, g + 8] = far[np.random.randint(len(far))]
    return np.exp2(a.ravel()).repeat(32)


def f64(x):
    return np.asarray(x).astype(np.float64)


def striped(idx):
    return np.tile(np.asarray(idx).reshape(-1, 16).T, (8, 1)).astype(np.uint16)


def unstriped(offs):
    return offs[:16].T.reshape(-1).astype(np.int64)


E2M1 = np.array([0.0, 0.5, 1.0, 1.5, 2.0, 3.0, 4.0, 6.0, -0.0, -0.5, -1.0, -1.5, -2.0, -3.0, -4.0, -6.0])


def pack_weight(w, fmt):
    k, n = w.shape
    w = f64(np.asarray(w, np.float32).astype(ml_dtypes.bfloat16)).reshape(k // 32, 32, n)
    amax = np.abs(w).max(1)
    if fmt == "e4m3":
        byte = np.frexp(amax)[1] - 1 + 127 - 7
    else:
        mant, ex = np.frexp(amax / 6.0)
        byte = np.where(mant > 0.5, ex, ex - 1) + 127
    byte = np.clip(np.where(amax > 0, byte, 1), 1, 254)
    scaled = (w * np.exp2(127.0 - byte)[:, None, :]).reshape(k, n).astype(np.float32)
    by_word = np.ascontiguousarray(scaled.reshape(k // 512, 128, 4, n).transpose(0, 1, 3, 2))
    if fmt == "e4m3":
        words = by_word.astype(ml_dtypes.float8_e4m3fn).view(np.uint8)
    else:
        c = by_word.astype(ml_dtypes.float4_e2m1fn).view(np.uint8) & 0xF
        words = (c[..., 0::2] | (c[..., 1::2] << 4)).reshape(k // 512, 128, 2 * n)
    return np.ascontiguousarray(words), np.ascontiguousarray(byte.astype(np.uint8).reshape(k // 512, 16, n))


def unpack_weight(words, scales, fmt):
    g, _, n = scales.shape
    words = np.ascontiguousarray(words).reshape(g, 128, n, -1)
    if fmt == "e4m3":
        vals = words.view(ml_dtypes.float8_e4m3fn).astype(np.float64)
    else:
        nib = np.empty((g, 128, n, 4), np.uint8)
        nib[..., 0::2] = words & 0xF
        nib[..., 1::2] = words >> 4
        vals = E2M1[nib]
    vals = vals * np.repeat(np.exp2(scales.astype(np.float64) - 127.0), 8, axis=1)[..., None]
    return vals.transpose(0, 1, 3, 2).reshape(g * 512, n)


def sigmoid(v):
    return 1.0 / (1.0 + np.exp(-v))


D, E, T, I, G, U, Q = 512, 512, 4096, 1024, 64, 512, 128


def setup_inputs():
    n = np.random.standard_normal
    idx = np.random.permutation(T)[:I]
    idx2 = np.random.permutation(U)[:G]
    fd = mx_kscale(D)
    fe = mx_kscale(E)
    keysp = pack_weight(n((D, T)) / fd[:, None], "e4m3")
    valsp = pack_weight(n((E, T)) / fe[:, None], "e4m3")
    return {
        "query": (n((D, Q)) * 0.7 / np.sqrt(D) * fd[:, None]).astype(np.float32),
        "keys_words": keysp[0],
        "keys_scales": keysp[1],
        "ptab": (n((Q, U)) * 1.0).astype(np.float32),
        "gout": (n((E, Q)) * 1 / np.sqrt(E) * fe[:, None]).astype(np.float32),
        "vals_words": valsp[0],
        "vals_scales": valsp[1],
        "lam": (np.random.uniform(0.5, 1.5, (Q, 1))).astype(np.float32),
        "dquery": (n((D, Q)) * 1.0 / np.sqrt(D) * fd[:, None]).astype(np.float32),
        "base": (0.5 * n((Q, G))).astype(np.float32),
        "offs": striped(idx),
        "offs2": striped(idx2),
    }


def reference(query, keys_words, keys_scales, ptab, gout, vals_words, vals_scales, lam, dquery, base, offs, offs2):
    idx = unstriped(offs)
    idx2 = unstriped(offs2)
    keysu = unpack_weight(keys_words, keys_scales, "e4m3")
    valsu = unpack_weight(vals_words, vals_scales, "e4m3")
    queryq = mxq(f64(query), 0, "e4m3")
    keysidxg = keysu[:, idx]
    a = queryq.T @ keysidxg
    dqueryq = mxq(f64(dquery), 0, "e4m3")
    ta = dqueryq.T @ keysidxg
    b = a.reshape(Q, G, I // G).mean(axis=2)
    tp = f64(ptab)[:, idx2] * f64(lam)
    gt = sigmoid(tp + b)
    gr = np.repeat(gt, I // G, axis=1)
    r = np.exp(a - np.max(a, axis=1, keepdims=True))
    p = r * gr
    z = np.sum(p, axis=1, keepdims=True)
    goutq = mxq(f64(gout), 0, "e4m3")
    valsidxg = valsu[:, idx]
    c0 = goutq.T @ valsidxg
    dz = np.sum(p * c0, axis=1, keepdims=True) / np.square(z) * (-1.0)
    dp = 1.0 / z * c0 + dz
    dgr = dp * r
    dgt = dgr.reshape(Q, G, I // G).sum(axis=2)
    xb = ta.reshape(Q, G, I // G).mean(axis=2)
    xgt = xb * gt * (1.0 - gt)
    xgr = np.repeat(xgt, I // G, axis=1)
    xr = ta * r
    xp = xr * gr + xgr * r
    xz = np.sum(xp, axis=1, keepdims=True)
    xdz = (np.sum(xp * c0, axis=1, keepdims=True) - xz * z * 2.0 * np.sum(p * c0, axis=1, keepdims=True) / np.square(z)) / np.square(z) * (-1.0)
    xdp = xz * 1.0 / np.square(z) * (-1.0) * c0 + xdz
    xdgr = xdp * r + xr * dp
    xdgt = xdgr.reshape(Q, G, I // G).sum(axis=2)
    xdtp = (xdgt * gt + xgt * dgt) * (1.0 - gt) + xgt * (-1.0) * dgt * gt
    y = xdtp * 64.0 + f64(base)
    return y

from contextlib import ExitStack

import concourse.mybir as mybir

D, T, I, G, U, Q = 512, 4096, 1024, 64, 512, 128
FLOPS = 3 * 2 * D * Q * I

F32 = mybir.dt.float32
BF16 = mybir.dt.bfloat16
I32 = mybir.dt.int32
U32 = mybir.dt.uint32
U16 = mybir.dt.uint16
U8 = mybir.dt.uint8
FP8X4 = mybir.dt.float8_e4m3fn_x4
ALU = mybir.AluOpType
ACT = mybir.ActivationFunctionType
AXIS = mybir.AxisListType

P = 128
PACK = 4
PAGE = I // G
HALF = 512
HALVES = I // HALF
GH = HALF // PAGE
LIST_COLS = HALF // 16
VAL_ROW0 = 4
SLABS = 4


def tile_attend_hvpagelift_kernel(tc, query, keys_words, keys_scales, ptab, gout, vals_words, vals_scales,
                                   lam, dquery, base, offs, offs2, out):
    nc = tc.nc
    with ExitStack() as ctx:
        sb = ctx.enter_context(tc.tile_pool(name="sb", bufs=1))
        ps = ctx.enter_context(tc.psum_pool(name="ps", bufs=1))

        def load_list(name, src, n):
            lst = sb.tile([P, n // 16], U16, name=name)
            nc.sync.dma_start(lst[:], src)
            return lst

        def zero_plane(name):
            plane = sb.tile([P, T], U8, name=name, align_bytes=64)
            nc.vector.memset(plane[:].bitcast(I32), 0)
            return plane

        def load_scales(plane, src, row0):
            for quad in range(4):
                first = 32 * quad + row0
                nc.sync.dma_start(plane[first:first + 4, :].bitcast(I32),
                                  src[0, 4 * quad:4 * quad + 4, :].bitcast(I32))

        def load_words(words, src, cols):
            nc.sync.dma_start(words[:, cols].bitcast(I32), src[0].rearrange("p t r -> p (t r)").bitcast(I32)[:, cols])

        def load_rows(name, src, tag):
            raw = sb.tile([P, PACK, Q], F32, name=name, tag=tag, align_bytes=64)
            nc.sync.dma_start(raw[:], src.rearrange("(p j) w -> p j w", j=PACK))
            return raw

        slots = load_list("slots", offs, I)
        pages = load_list("pages", offs2, G)
        q_raw = load_rows("q_raw", query, "rows_a")
        dq_raw = load_rows("dq_raw", dquery, "rows_b")

        warm_in = sb.tile([P, 1], F32, name="warm_in")
        nc.gpsimd.memset(warm_in[:], 0.0)
        warm = sb.tile([P, 1], F32, name="warm")
        nc.scalar.activation(warm[:], warm_in[:], ACT.Exp)

        key_plane = zero_plane("key_plane")
        load_scales(key_plane, keys_scales, 0)
        zeros = sb.tile([P, P], F32, name="zeros", tag="key_words", align_bytes=64)
        nc.vector.memset(zeros[:], 0.0)
        ident = sb.tile([P, P], F32, name="ident")
        nc.gpsimd.affine_select(out=ident[:], in_=zeros[:], pattern=[[-1, P]], compare_op=ALU.not_equal, fill=1.0,
                                base=0, channel_multiplier=1)
        val_plane = zero_plane("val_plane")
        key_words = sb.tile([P, T], U32, name="key_words", tag="key_words", align_bytes=64)
        load_words(key_words, keys_words, slice(0, T // 2))
        load_scales(val_plane, vals_scales, VAL_ROW0)
        load_words(key_words, keys_words, slice(T // 2, T))

        def quantise(name, raws):
            n = len(raws) * Q
            grouped = sb.tile([P, n, PACK], BF16, name=name + "_bf", tag=name + "_bf", align_bytes=64)
            for i, raw in enumerate(raws):
                nc.scalar.copy(grouped[:, i * Q:(i + 1) * Q, :], raw[:].rearrange("p j w -> p w j"))
            codes = sb.tile([P, n], U32, name=name + "_codes", align_bytes=64)
            scales = sb.tile([P, n], U8, name=name + "_scales", align_bytes=64)
            nc.vector.quantize_mx(out=codes[:].bitcast(FP8X4), scales=scales[:],
                                  in_=grouped[:].rearrange("p w j -> p (w j)"))
            return codes, scales

        def gather(name, window, lst, n, dtype, tag=None):
            got = sb.tile([P, n], dtype, name=name, tag=tag or name, align_bytes=64)
            nc.vector.tensor_copy(got[:], window[:].indirect(lst))
            return got

        def half_list(h):
            return slots[:, h * LIST_COLS:(h + 1) * LIST_COLS]

        def product(tag, codes, scales, col0, words, plane):
            bank = ps.tile([P, HALF], F32, name=tag, tag=tag)
            nc.tensor.matmul_mx(out=bank[:], lhsT=codes[:, col0:col0 + Q].bitcast(FP8X4),
                                lhsT_scale=scales[:, col0:col0 + Q], rhs=words[:].bitcast(FP8X4),
                                rhs_scale=plane, start=True, stop=True)
            return bank[:].rearrange("p (g j) -> p j g", j=PAGE)

        def page_sums(name, pair, tag_sum, tag_back):
            acc = ps.tile([P, P], F32, name=name + "_acc", tag=tag_sum)
            for j in range(PAGE):
                nc.tensor.matmul(acc[:], lhsT=pair[:, j, :, :].rearrange("p a g -> p (a g)"), rhs=ident[:],
                                 is_transpose=True, start=(j == 0), stop=(j == PAGE - 1))
            turned = sb.tile([P, P], F32, name=name + "_turned")
            nc.scalar.copy(turned[:], acc[:])
            sums = ps.tile([P, 2, G], F32, name=name + "_sums", tag=tag_back)
            nc.tensor.transpose(sums[:].rearrange("p a g -> p (a g)"), turned[:], ident[:])
            return sums

        key_bytes = gather("key_bytes", key_plane, slots[:], I, U8)
        q_codes, q_scales = quantise("q", [q_raw, dq_raw])
        g_raw = load_rows("g_raw", gout, "rows_a")
        val_words = sb.tile([P, T], U32, name="val_words", tag="rows_b", align_bytes=64)
        load_words(val_words, vals_words, slice(0, T))
        val_bytes = [gather("val_bytes0", val_plane, half_list(0), HALF, U8)]

        key_got = [gather("key_got%d" % h, key_words, half_list(h), HALF, U32) for h in range(HALVES)]
        scores = sb.tile([P, PAGE, 2, G], F32, name="scores")
        neg_max = [sb.tile([P, 1], F32, name="neg_max%d" % h) for h in range(HALVES)]
        for h in range(HALVES):
            plane = key_bytes[:, h * HALF:(h + 1) * HALF]
            a_bank = product("a%d" % h, q_codes, q_scales, 0, key_got[h], plane)
            t_bank = product("t%d" % h, q_codes, q_scales, Q, key_got[h], plane)
            cols = slice(h * GH, (h + 1) * GH)
            nc.vector.tensor_scalar(out=scores[:, :, 0, cols], in0=a_bank, scalar1=-1.0,
                                    scalar2=(neg_max[h - 1][:] if h else None), op0=ALU.mult, op1=ALU.min,
                                    accum_out=neg_max[h][:])
            nc.scalar.copy(scores[:, :, 1, cols], t_bank)

        val_bytes.append(gather("val_bytes1", val_plane, half_list(1), HALF, U8, tag="key_got0"))
        g_codes, g_scales = quantise("g", [g_raw])
        lifts = sb.tile([P, U], F32, name="lifts", tag="rows_a", align_bytes=64)
        nc.sync.dma_start(lifts[:], ptab)
        lam_col = sb.tile([P, 1], F32, name="lam_col", tag="q_bf", align_bytes=64)
        nc.sync.dma_start(lam_col[:], lam)
        terms = sb.tile([P, 3, G], F32, name="terms", tag="g_bf", align_bytes=64)
        nc.sync.dma_start(terms[:, 2, :], base)

        weights = sb.tile([P, PAGE, 2, G], F32, name="weights")
        for js in (slice(0, PAGE // 2), slice(PAGE // 2, PAGE)):
            nc.scalar.activation(weights[:, js, 0, :], scores[:, js, 0, :], ACT.Exp, bias=neg_max[HALVES - 1][:], scale=-1.0)
            nc.vector.tensor_tensor(weights[:, js, 1, :], weights[:, js, 0, :], scores[:, js, 1, :], ALU.mult)
        warm2 = sb.tile([P, 1], F32, name="warm2")
        nc.scalar.activation(warm2[:], weights[:, PAGE - 1, 0, 0:1], ACT.Sigmoid)

        def value_product(h):
            vw = gather("val_got%d" % h, val_words, half_list(h), HALF, U32)
            return product("c%d" % h, g_codes, g_scales, 0, vw, val_bytes[h][VAL_ROW0:P, :])

        c_banks = [value_product(0)]

        score_sums = page_sums("score", scores, "x", "y")
        means = sb.tile([P, 2, G], F32, name="means")
        nc.scalar.activation(means[:], score_sums[:], ACT.Copy, scale=1.0 / PAGE)
        picked = gather("picked", lifts, pages[:], G, F32)
        arg = sb.tile([P, G], F32, name="arg")
        nc.vector.scalar_tensor_tensor(arg[:], picked[:], lam_col[:], means[:, 0, :], ALU.mult, ALU.subtract)
        gates = sb.tile([P, 2, G], F32, name="gates")
        rest = sb.tile([P, G], F32, name="rest")
        nc.scalar.activation(gates[:, 1, :], arg[:], ACT.Sigmoid)
        nc.scalar.activation(rest[:], arg[:], ACT.Sigmoid, scale=-1.0)
        slope = sb.tile([P, G], F32, name="slope")
        nc.gpsimd.tensor_tensor(slope[:], gates[:, 1, :], rest[:], ALU.mult)
        nc.gpsimd.tensor_tensor(gates[:, 0, :], means[:, 1, :], slope[:], ALU.mult)
        diff = sb.tile([P, G], F32, name="diff")
        nc.scalar.activation(diff[:], gates[:, 1, :], ACT.Copy, scale=-2.0, bias=1.0)
        neg_slope = sb.tile([P, G], F32, name="neg_slope")
        nc.scalar.activation(neg_slope[:], slope[:], ACT.Copy, scale=-64.0)
        bend = sb.tile([P, G], F32, name="bend")
        nc.gpsimd.tensor_tensor(bend[:], means[:, 1, :], diff[:], ALU.mult)

        c_banks.append(value_product(1))
        mixed = sb.tile([P, PAGE, 2, G], F32, name="mixed")
        step = PAGE // SLABS
        for s in range(SLABS):
            js = slice(s * step, (s + 1) * step)
            for h in range(HALVES):
                cols = slice(h * GH, (h + 1) * GH)
                nc.vector.tensor_tensor(mixed[:, js, :, cols], weights[:, js, :, cols],
                                        c_banks[h][:, js, :].unsqueeze(2).to_broadcast([P, step, 2, GH]), ALU.mult)

        wsum = page_sums("weight", weights, "a0", "a1")
        junk_z = sb.tile([P, G], F32, name="junk_z")
        z = sb.tile([P, 1], F32, name="z")
        nc.vector.scalar_tensor_tensor(junk_z[:], wsum[:, 0, :], 1.0, gates[:, 1, :], ALU.mult, ALU.mult, accum_out=z[:])
        junk_xz = sb.tile([P, 2, G], F32, name="junk_xz")
        xz = sb.tile([P, 1], F32, name="xz")
        nc.vector.scalar_tensor_tensor(junk_xz[:], wsum[:], 1.0, gates[:], ALU.mult, ALU.mult, accum_out=xz[:])
        pp = sb.tile([P, 2, G], F32, name="pp")
        nc.vector.tensor_tensor(pp[:], wsum[:], neg_slope[:].unsqueeze(1).to_broadcast([P, 2, G]), ALU.mult)
        iz = sb.tile([P, 1], F32, name="iz")
        nc.vector.reciprocal(iz[:], z[:])
        e1 = sb.tile([P, 1], F32, name="e1")
        nc.vector.tensor_scalar(e1[:], xz[:], iz[:], None, ALU.mult)
        e2 = sb.tile([P, 1], F32, name="e2")
        nc.vector.tensor_scalar(e2[:], xz[:], iz[:], 2.0, ALU.mult, ALU.mult)
        pw = sb.tile([P, 2, G], F32, name="pw")
        nc.vector.tensor_scalar(pw[:, 1, :], neg_slope[:], iz[:], -1.0, ALU.mult, ALU.mult)
        gates2 = sb.tile([P, 2, G], F32, name="gates2")
        nc.vector.tensor_scalar(gates2[:], gates[:], iz[:], iz[:], ALU.mult, ALU.mult)
        nc.vector.scalar_tensor_tensor(pw[:, 0, :], bend[:], e1[:], pw[:, 1, :], ALU.subtract, ALU.mult)
        p2a = sb.tile([P, G], F32, name="p2a")
        nc.vector.scalar_tensor_tensor(p2a[:], bend[:], e2[:], pp[:, 0, :], ALU.subtract, ALU.mult)
        p2 = sb.tile([P, G], F32, name="p2")
        nc.vector.tensor_tensor(p2[:], p2a[:], pp[:, 1, :], ALU.add)

        msum = page_sums("mixed", mixed, "t0", "t1")

        junk_c = sb.tile([P, G], F32, name="junk_c")
        c = sb.tile([P, 1], F32, name="c")
        nc.vector.scalar_tensor_tensor(junk_c[:], msum[:, 0, :], 1.0, gates2[:, 1, :], ALU.mult, ALU.mult, accum_out=c[:])
        junk_f = sb.tile([P, 2, G], F32, name="junk_f")
        f = sb.tile([P, 1], F32, name="f")
        nc.vector.scalar_tensor_tensor(junk_f[:], msum[:], 1.0, gates2[:], ALU.mult, ALU.mult, accum_out=f[:])
        direct = sb.tile([P, 2, G], F32, name="direct")
        nc.vector.tensor_tensor(direct[:], msum[:], pw[:], ALU.mult)
        nc.vector.scalar_tensor_tensor(terms[:, 0, :], p2[:], c[:], direct[:, 1, :], ALU.mult, ALU.add)
        nc.vector.scalar_tensor_tensor(terms[:, 1, :], pp[:, 0, :], f[:], direct[:, 0, :], ALU.mult, ALU.add)
        result = sb.tile([P, G], F32, name="result")
        nc.vector.tensor_reduce(result[:], terms[:].rearrange("p a g -> p g a"), AXIS.X, ALU.add)
        nc.sync.dma_start(out, result[:])
